import numpy as np
import ml_dtypes

BF16 = ml_dtypes.bfloat16


def bf(x):
    return np.asarray(x, np.float32).astype(BF16)


def f32(x):
    return np.asarray(x, np.float32)


def f64(x):
    return np.asarray(x).astype(np.float64)


def striped(idx):
    return np.tile(idx.reshape(-1, 16).T, (8, 1))


S, K, M, N = 256, 128, 512, 64


def setup_inputs():
    return {"base": bf(np.random.standard_normal((M, S))), "x": bf(np.random.standard_normal((K, N))), "w": bf(np.random.standard_normal((K, M)) / np.sqrt(K)), "s": f32(0.5 + np.random.random_sample((M, 1))), "b": f32(0.5 * np.random.standard_normal((M, 1))), "offs": striped(np.random.permutation(S)[:N])}


def reference(base, x, w, s, b, offs):
    idx = offs[:16].T.reshape(-1)
    z = f64(base).copy()
    z[:, idx] += f64(w).T @ f64(x)
    return z * f64(s) + f64(b)

@@ -1,0 +1,59 @@
+import concourse.mybir as mybir
+from concourse.masks import make_identity
+
+BF16, F32, U16 = mybir.dt.bfloat16, mybir.dt.float32, mybir.dt.uint16
+MULT, ADD = mybir.AluOpType.mult, mybir.AluOpType.add
+IDENTITY = mybir.ActivationFunctionType.Identity
+
+FLOPS = 2 * 128 * 512 * 64
+
+
+def tile_scatter_matmul_kernel(tc, base, x, w, s, b, offs, out):
+    nc = tc.nc
+    P = 128
+    M, S = base.shape
+    K, N = x.shape
+    A = M // P
+
+    with (
+        tc.tile_pool(name="held", bufs=1) as held,
+        tc.psum_pool(name="windows", bufs=1) as windows,
+    ):
+        offsets = held.tile([P, N // 16], U16)
+        base_t = held.tile([P, A, S], BF16)
+        w_t = held.tile([P, M], BF16)
+        x_t = held.tile([P, N], BF16)
+        s_t = held.tile([P, A], F32)
+        b_t = held.tile([P, A], F32)
+        ident = held.tile([P, P], BF16)
+
+        nc.sync.dma_start(base_t[:], base.rearrange("(a p) t -> p a t", p=P))
+        nc.sync.dma_start(w_t[:], w)
+        nc.sync.dma_start(x_t[:], x)
+        nc.sync.dma_start(offsets[:], offs)
+        nc.sync.dma_start(s_t[:], s.rearrange("(a p) o -> p (a o)", p=P))
+        nc.sync.dma_start(b_t[:], b.rearrange("(a p) o -> p (a o)", p=P))
+        make_identity(nc, ident[:])
+
+        window = [windows.tile([P, S], F32, name=f"window{a}") for a in range(A)]
+        for a in range(A):
+            nc.tensor.matmul(window[a][:], ident[:], base_t[:, a, :], start=True, stop=False)
+
+        for a in range(A):
+            nc.tensor.matmul(
+                window[a][:].indirect(offsets[:]),
+                w_t[:, a * P : (a + 1) * P],
+                x_t[:],
+                start=False,
+                stop=True,
+            )
+
+        for a in range(A):
+            out_t = held.tile([P, S], F32, name=f"out{a}")
+            out_rows = out[a * P : (a + 1) * P, :]
+            if a % 2 == 0:
+                nc.vector.tensor_scalar(out_t[:], window[a][:], s_t[:, a : a + 1], b_t[:, a : a + 1], MULT, ADD)
+                nc.sync.dma_start(out_rows, out_t[:])
+            else:
+                nc.scalar.activation(out_t[:], window[a][:], IDENTITY, bias=b_t[:, a : a + 1], scale=s_t[:, a : a + 1])
+                nc.scalar.dma_start(out_rows, out_t[:])

@@ -27,12 +27,12 @@ def tile_scatter_matmul_kernel(tc, base, x, w, s, b, offs, out):
         b_t = held.tile([P, A], F32)
         ident = held.tile([P, P], BF16)
 
-        nc.sync.dma_start(base_t[:], base.rearrange("(a p) t -> p a t", p=P))
+        nc.sync.dma_start(base_t[:], base.rearrange("(p a) t -> p a t", a=A))
         nc.sync.dma_start(w_t[:], w)
         nc.sync.dma_start(x_t[:], x)
         nc.sync.dma_start(offsets[:], offs)
-        nc.sync.dma_start(s_t[:], s.rearrange("(a p) o -> p (a o)", p=P))
-        nc.sync.dma_start(b_t[:], b.rearrange("(a p) o -> p (a o)", p=P))
+        nc.sync.dma_start(s_t[:], s.rearrange("(p a) o -> p (a o)", a=A))
+        nc.sync.dma_start(b_t[:], b.rearrange("(p a) o -> p (a o)", a=A))
         make_identity(nc, ident[:])
 
         window = [windows.tile([P, S], F32, name=f"window{a}") for a in range(A)]
@@ -42,7 +42,7 @@ def tile_scatter_matmul_kernel(tc, base, x, w, s, b, offs, out):
         for a in range(A):
             nc.tensor.matmul(
                 window[a][:].indirect(offsets[:]),
-                w_t[:, a * P : (a + 1) * P],
+                w_t[:, a:M:A],
                 x_t[:],
                 start=False,
                 stop=True,
@@ -50,7 +50,7 @@ def tile_scatter_matmul_kernel(tc, base, x, w, s, b, offs, out):
 
         for a in range(A):
             out_t = held.tile([P, S], F32, name=f"out{a}")
-            out_rows = out[a * P : (a + 1) * P, :]
+            out_rows = out.rearrange("(p a) t -> p a t", a=A)[:, a, :]
             if a % 2 == 0:
                 nc.vector.tensor_scalar(out_t[:], window[a][:], s_t[:, a : a + 1], b_t[:, a : a + 1], MULT, ADD)
                 nc.sync.dma_start(out_rows, out_t[:])

@@ -5,6 +5,8 @@ BF16, F32, U16 = mybir.dt.bfloat16, mybir.dt.float32, mybir.dt.uint16
 MULT, ADD = mybir.AluOpType.mult, mybir.AluOpType.add
 IDENTITY = mybir.ActivationFunctionType.Identity
 
+WARM_UPS = 4
+
 FLOPS = 2 * 128 * 512 * 64
 
 
@@ -34,6 +36,17 @@ def tile_scatter_matmul_kernel(tc, base, x, w, s, b, offs, out):
         nc.sync.dma_start(s_t[:], s.rearrange("(p a) o -> p (a o)", a=A))
         nc.sync.dma_start(b_t[:], b.rearrange("(p a) o -> p (a o)", a=A))
         make_identity(nc, ident[:])
+
+        table_in = held.tile([P, 1], F32)
+        table_out = held.tile([P, 1], F32)
+        nc.vector.memset(table_in[:], 0.0)
+        nc.scalar.activation(table_out[:], table_in[:], IDENTITY)
+
+        zeros = held.tile([P, 512], BF16)
+        warm_bank = windows.tile([P, 512], F32)
+        nc.vector.memset(zeros[:], 0.0)
+        for i in range(WARM_UPS):
+            nc.tensor.matmul(warm_bank[:], zeros[:, 0:P], zeros[:], start=True, stop=True)
 
         window = [windows.tile([P, S], F32, name=f"window{a}") for a in range(A)]
         for a in range(A):

@@ -5,7 +5,7 @@ BF16, F32, U16 = mybir.dt.bfloat16, mybir.dt.float32, mybir.dt.uint16
 MULT, ADD = mybir.AluOpType.mult, mybir.AluOpType.add
 IDENTITY = mybir.ActivationFunctionType.Identity
 
-WARM_UPS = 4
+WARM_UPS = 6
 
 FLOPS = 2 * 128 * 512 * 64
 
@@ -29,7 +29,9 @@ def tile_scatter_matmul_kernel(tc, base, x, w, s, b, offs, out):
         b_t = held.tile([P, A], F32)
         ident = held.tile([P, P], BF16)
 
-        nc.sync.dma_start(base_t[:], base.rearrange("(p a) t -> p a t", a=A))
+        base_rows = base.rearrange("(p a) t -> p a t", a=A)
+        for h in (slice(0, A // 2), slice(A // 2, A)):
+            nc.sync.dma_start(base_t[:, h, :], base_rows[:, h, :])
         nc.sync.dma_start(w_t[:], w)
         nc.sync.dma_start(x_t[:], x)
         nc.sync.dma_start(offsets[:], offs)
@@ -37,14 +39,11 @@ def tile_scatter_matmul_kernel(tc, base, x, w, s, b, offs, out):
         nc.sync.dma_start(b_t[:], b.rearrange("(p a) o -> p (a o)", a=A))
         make_identity(nc, ident[:])
 
-        table_in = held.tile([P, 1], F32)
+        zeros = held.tile([P, S], BF16)
         table_out = held.tile([P, 1], F32)
-        nc.vector.memset(table_in[:], 0.0)
-        nc.scalar.activation(table_out[:], table_in[:], IDENTITY)
-
-        zeros = held.tile([P, 512], BF16)
-        warm_bank = windows.tile([P, 512], F32)
+        warm_bank = windows.tile([P, S], F32)
         nc.vector.memset(zeros[:], 0.0)
+        nc.scalar.activation(table_out[:], zeros[:, 0:1], IDENTITY)
         for i in range(WARM_UPS):
             nc.tensor.matmul(warm_bank[:], zeros[:, 0:P], zeros[:], start=True, stop=True)
 

import concourse.mybir as mybir
from concourse.masks import make_identity

BF16, F32, U16 = mybir.dt.bfloat16, mybir.dt.float32, mybir.dt.uint16
MULT, ADD = mybir.AluOpType.mult, mybir.AluOpType.add
IDENTITY = mybir.ActivationFunctionType.Identity

WARM_UPS = 6

FLOPS = 2 * 128 * 512 * 64


def tile_scatter_matmul_kernel(tc, base, x, w, s, b, offs, out):
    nc = tc.nc
    P = 128
    M, S = base.shape
    K, N = x.shape
    A = M // P

    with (
        tc.tile_pool(name="held", bufs=1) as held,
        tc.psum_pool(name="windows", bufs=1) as windows,
    ):
        offsets = held.tile([P, N // 16], U16)
        base_t = held.tile([P, A, S], BF16)
        w_t = held.tile([P, M], BF16)
        x_t = held.tile([P, N], BF16)
        s_t = held.tile([P, A], F32)
        b_t = held.tile([P, A], F32)
        ident = held.tile([P, P], BF16)

        base_rows = base.rearrange("(p a) t -> p a t", a=A)
        for h in (slice(0, A // 2), slice(A // 2, A)):
            nc.sync.dma_start(base_t[:, h, :], base_rows[:, h, :])
        nc.sync.dma_start(w_t[:], w)
        nc.sync.dma_start(x_t[:], x)
        nc.sync.dma_start(offsets[:], offs)
        nc.sync.dma_start(s_t[:], s.rearrange("(p a) o -> p (a o)", a=A))
        nc.sync.dma_start(b_t[:], b.rearrange("(p a) o -> p (a o)", a=A))
        make_identity(nc, ident[:])

        zeros = held.tile([P, S], BF16)
        table_out = held.tile([P, 1], F32)
        warm_bank = windows.tile([P, S], F32)
        nc.vector.memset(zeros[:], 0.0)
        nc.scalar.activation(table_out[:], zeros[:, 0:1], IDENTITY)
        for i in range(WARM_UPS):
            nc.tensor.matmul(warm_bank[:], zeros[:, 0:P], zeros[:], start=True, stop=True)

        window = [windows.tile([P, S], F32, name=f"window{a}") for a in range(A)]
        for a in range(A):
            nc.tensor.matmul(window[a][:], ident[:], base_t[:, a, :], start=True, stop=False)

        for a in range(A):
            nc.tensor.matmul(
                window[a][:].indirect(offsets[:]),
                w_t[:, a:M:A],
                x_t[:],
                start=False,
                stop=True,
            )

        for a in range(A):
            out_t = held.tile([P, S], F32, name=f"out{a}")
            out_rows = out.rearrange("(p a) t -> p a t", a=A)[:, a, :]
            if a % 2 == 0:
                nc.vector.tensor_scalar(out_t[:], window[a][:], s_t[:, a : a + 1], b_t[:, a : a + 1], MULT, ADD)
                nc.sync.dma_start(out_rows, out_t[:])
            else:
                nc.scalar.activation(out_t[:], window[a][:], IDENTITY, bias=b_t[:, a : a + 1], scale=s_t[:, a : a + 1])
                nc.scalar.dma_start(out_rows, out_t[:])
